import numpy as np
import ml_dtypes


def mxq(x, axis, fmt="e4m3"):
    dtype, down = {"e4m3": (ml_dtypes.float8_e4m3fn, 7), "e5m2": (ml_dtypes.float8_e5m2, 14)}[fmt]
    v = np.moveaxis(np.asarray(x, np.float32).astype(ml_dtypes.bfloat16).astype(np.float64), axis, -1)
    blocks = v.reshape(v.shape[:-1] + (-1, 32))
    amax = np.abs(blocks).max(-1, keepdims=True)
    byte = np.maximum(np.where(amax > 0, np.frexp(amax)[1] - 1 + 127, 0) - down, 1)
    scale = np.exp2(byte - 127.0)
    codes = (blocks / scale).astype(np.float32).astype(dtype).astype(np.float64)
    return np.moveaxis((codes * scale).reshape(v.shape), -1, axis)


WIDE = False


def mx_kscale(k):
    if not WIDE:
        return np.ones(k)
    levels = np.array([10, -10, 5, -5, 0])
    if k % 512:
        return np.exp2(np.random.permutation(np.resize(levels, k // 32))).repeat(32)
    a = np.empty((k // 512, 16))
    for p in range(k // 512):
        a[p, :8] = np.random.permutation(np.resize(levels, 8))
        for g in range(8):
            far = levels[np.abs(levels - a[p, g]) >= 10]
            a[p, g + 8] = far[np.random.randint(len(far))]
    return np.exp2(a.ravel()).repeat(32)


def f64(x):
    return np.asarray(x).astype(np.float64)


def striped(idx):
    return np.tile(idx.reshape(-1, 16).T, (8, 1)).astype(np.uint16)


def unstriped(offs):
    return offs[:16].T.reshape(-1).astype(np.int64)


def pack_weight(w):
    k, n = w.shape
    w = f64(np.asarray(w, np.float32).astype(ml_dtypes.bfloat16)).reshape(k // 32, 32, n)
    amax = np.abs(w).max(1)
    byte = np.clip(np.where(amax > 0, np.frexp(amax)[1] - 1 + 127 - 7, 1), 1, 254)
    scaled = (w * np.exp2(127.0 - byte)[:, None, :]).reshape(k, n).astype(np.float32)
    words = np.ascontiguousarray(scaled.reshape(k // 512, 128, 4, n).transpose(0, 1, 3, 2)).astype(ml_dtypes.float8_e4m3fn).view(np.uint8)
    return words, np.ascontiguousarray(byte.astype(np.uint8).reshape(k // 512, 16, n))


def unpack_weight(words, scales):
    g, p, n, _ = words.shape
    vals = np.ascontiguousarray(words).view(ml_dtypes.float8_e4m3fn).astype(np.float64) * np.repeat(np.exp2(scales.astype(np.float64) - 127.0), 8, axis=1)[..., None]
    return vals.transpose(0, 1, 3, 2).reshape(g * 512, n)


def planes(y):
    n, m = y.shape
    v = y.astype(np.float32).astype(ml_dtypes.bfloat16).astype(np.float64).reshape(n // 32, 32, m)
    top = np.abs(v).max(1)
    byte = np.clip(np.where(top > 0, np.frexp(top)[1] - 1 + 127 - 7, 1), 1, 254)
    codes = (v * np.exp2(127.0 - byte)[:, None, :]).reshape(n, m).astype(np.float32).astype(ml_dtypes.float8_e4m3fn).view(np.uint8)
    words = codes.reshape(n // 512, 128, 4, m).transpose(0, 1, 3, 2)
    return np.ascontiguousarray(words), np.ascontiguousarray(byte.astype(np.uint8).reshape(n // 512, 16, m))


K, T, S, V, D, N = 1024, 4096, 1024, 256, 3, 512
P = 2 ** 7


def setup_inputs():
    n = np.random.standard_normal
    s = mx_kscale(K)[:, None]
    packed_xT = pack_weight(n((K, T)) * s)
    return {
        "x_words": packed_xT[0],
        "x_scales": packed_xT[1],
        "w0": (n((K, N)) / np.sqrt(K) / s).astype(np.float32),
        "w1": (n((K, N)) / np.sqrt(K) / s).astype(np.float32),
        "w2": (n((K, N)) / np.sqrt(K) / s).astype(np.float32),
        "w3": (n((K, N)) / np.sqrt(K) / s).astype(np.float32),
        "gate": (np.tile(np.random.uniform(0.2, 1.0, (D, 1, V)), (1, P, 1))).astype(np.float32),
        "offs": striped(np.random.permutation(T)[:S]),
    }


def reference(x_words, x_scales, w0, w1, w2, w3, gate, offs):
    xq = unpack_weight(x_words, x_scales)[:, unstriped(offs)]
    y0 = mxq(f64(w0), 0, "e4m3").T @ xq[:, :V]
    y1 = mxq(f64(w1), 0, "e4m3").T @ xq[:, V:2 * V]
    y2 = mxq(f64(w2), 0, "e4m3").T @ xq[:, 2 * V:3 * V]
    y3 = mxq(f64(w3), 0, "e4m3").T @ xq[:, 3 * V:4 * V]
    out_0 = y0 + y1 * f64(gate)[0, :1] + y2 * f64(gate)[1, :1] + y3 * f64(gate)[2, :1]
    return (out_0,) + planes(out_0)

@@ -1,0 +1,234 @@
+from contextlib import ExitStack
+
+import concourse.mybir as mybir
+from concourse.masks import make_identity
+
+K, T, S, V, D, N = 1024, 4096, 1024, 256, 3, 512
+FLOPS = 2 * (D + 1) * K * N * V
+
+F32 = mybir.dt.float32
+BF16 = mybir.dt.bfloat16
+I32 = mybir.dt.int32
+U32 = mybir.dt.uint32
+U16 = mybir.dt.uint16
+U8 = mybir.dt.uint8
+FP8X4 = mybir.dt.float8_e4m3fn_x4
+MULT = mybir.AluOpType.mult
+ADD = mybir.AluOpType.add
+
+P = 128
+PACK = 4
+K_PASS = P * PACK
+PASSES = K // K_PASS
+HALVES = V // P
+QUADS = 4
+RAW_BUFS = 4
+SCALAR_COLS = 384
+SCALAR_COLS_LAST = 256
+
+
+def tile_picked_zrgcn_none_po_kernel(
+    tc, x_words, x_scales, w0, w1, w2, w3, gate, offs, out_0, out_1, out_2
+):
+    nc = tc.nc
+    with ExitStack() as ctx:
+        keep = ctx.enter_context(tc.tile_pool(name="keep", bufs=1))
+        ring = ctx.enter_context(tc.tile_pool(name="ring", bufs=RAW_BUFS))
+        psum = ctx.enter_context(tc.psum_pool(name="psum", bufs=1))
+
+        offsets = keep.tile([P, S // 16], U16, name="offsets")
+        nc.sync.dma_start(offsets[:], offs)
+
+        scale_table = keep.tile([P, T], U8, name="scale_table", align_bytes=64)
+        nc.vector.memset(scale_table[:].bitcast(I32), 0)
+        nc.scalar.dma_start(
+            out=scale_table[:].bitcast(I32)[0:P:4, :],
+            in_=x_scales.bitcast(I32).rearrange("a q c -> q a c"),
+        )
+
+        gate_rows = keep.tile([P, V], F32, name="gate_rows")
+        nc.vector.memset(gate_rows[:], 0.0)
+        nc.scalar.dma_start(out=gate_rows[0:D, :], in_=gate[:, 0, :])
+
+        x_planes = keep.tile([P, PASSES, S], U8, name="x_planes", align_bytes=64)
+        nc.vector.memset(x_planes[:].rearrange("p a s -> p (a s)").bitcast(I32), 0)
+
+        word_tables = []
+        for a in range(PASSES):
+            table = keep.tile([P, T], I32, name="word_table%d" % a, align_bytes=64)
+            nc.sync.dma_start(out=table[:], in_=x_words[a].rearrange("p n t -> p (n t)").bitcast(I32))
+            word_tables.append(table)
+
+        identity = keep.tile([P, P], F32, name="identity")
+        make_identity(nc, identity[:])
+
+        picked_scales = keep.tile([P, S], U8, name="picked_scales", align_bytes=64)
+        nc.vector.tensor_copy(picked_scales[:], scale_table[:].indirect(offsets[:]))
+        for q in range(QUADS):
+            nc.gpsimd.dma_start(
+                out=x_planes[:].rearrange("p a s -> p (a s)").bitcast(I32)[32 * q : 32 * q + 4, :],
+                in_=picked_scales[:].bitcast(I32)[32 * q : 32 * (q + 1) : 4, :],
+            )
+
+        x_codes = []
+        for a in range(PASSES):
+            picked = keep.tile([P, S], U32, name="x_codes%d" % a, align_bytes=64)
+            nc.vector.tensor_copy(picked[:], word_tables[a][:].bitcast(U32).indirect(offsets[:]))
+            x_codes.append(picked)
+
+        gate_bank = psum.tile([P, HALVES, P], F32, name="gate_bank")
+        for h in range(HALVES):
+            nc.tensor.transpose(gate_bank[:, h, :], gate_rows[:, h * P : (h + 1) * P], identity[:])
+        gate_cols = keep.tile([P, HALVES, D], F32, name="gate_cols")
+        nc.scalar.copy(out=gate_cols[:], in_=gate_bank[:, :, 0:D])
+
+        def load_rows(w, a, cols):
+            width = cols.stop - cols.start
+            raw = ring.tile([P, PACK, width], F32, name="raw")
+            rows = w[a * K_PASS : (a + 1) * K_PASS, :].rearrange("(p j) c -> p j c", j=PACK)
+            nc.sync.dma_start(out=raw[:], in_=rows[:, :, cols])
+            return raw
+
+        def copy_on(engine, out, in_):
+            if engine == "scalar":
+                nc.scalar.copy(out=out, in_=in_)
+            else:
+                nc.vector.tensor_copy(out=out, in_=in_)
+
+        def quantize(codes, scales, in_):
+            nc.vector.quantize_mx(out=codes.bitcast(FP8X4), scales=scales, in_=in_)
+
+        sums = [keep.tile([P, PACK, P], F32, name="sums%d" % h) for h in range(HALVES)]
+        for d, w in ((1, w1), (2, w2), (3, w3)):
+            banks = [psum.tile([P, N], F32, name="part", tag="part%d_%d" % (d % 2, h)) for h in range(HALVES)]
+            for a in range(PASSES):
+                raw = load_rows(w, a, slice(0, N))
+                codes = keep.tile([P, N], U32, name="w%d_codes%d" % (d, a), align_bytes=64)
+                scales = keep.tile([P, N], U8, name="w%d_scales%d" % (d, a), align_bytes=64)
+                split = SCALAR_COLS_LAST if (d, a) == (D, PASSES - 1) else SCALAR_COLS
+                shares = []
+                for engine, cols in (("vector", slice(split, N)), ("scalar", slice(0, split))):
+                    width = cols.stop - cols.start
+                    grouped = keep.tile([P, width, PACK], BF16, name="w%d_%d_%s" % (d, a, engine), align_bytes=64)
+                    copy_on(
+                        engine,
+                        grouped[:].rearrange("p (c i) j -> p c j i", i=4),
+                        raw[:, :, cols].rearrange("p j (c i) -> p c j i", i=4),
+                    )
+                    shares.append((cols, grouped))
+                for cols, grouped in shares:
+                    quantize(codes[:, cols], scales[:, cols], grouped[:].rearrange("p c j -> p (c j)"))
+                for h in range(HALVES):
+                    picked = slice(d * V + h * P, d * V + (h + 1) * P)
+                    nc.tensor.matmul_mx(
+                        out=banks[h][:],
+                        lhsT=x_codes[a][:, picked].bitcast(FP8X4),
+                        lhsT_scale=x_planes[:, a, picked],
+                        rhs=codes[:].bitcast(FP8X4),
+                        rhs_scale=scales[:],
+                        start=(a == 0),
+                        stop=(a == PASSES - 1),
+                    )
+            for h in range(HALVES):
+                product = banks[h][:].rearrange("p (m t) -> p t m", t=PACK)
+                weight = gate_cols[:, h, d - 1 : d]
+                if d == 1:
+                    nc.vector.tensor_scalar(out=sums[h][:], in0=product, scalar1=weight, scalar2=None, op0=MULT)
+                else:
+                    nc.vector.scalar_tensor_tensor(
+                        out=sums[h][:], in0=product, scalar=weight, in1=sums[h][:], op0=MULT, op1=ADD
+                    )
+
+        turned_banks = []
+        for h in range(HALVES):
+            bank = psum.tile([P, PACK, P], F32, name="turned", tag="part0_%d" % h)
+            for t in range(PACK):
+                nc.tensor.transpose(bank[:, t, :], sums[h][:, t, :], identity[:])
+            turned_banks.append(bank)
+
+        own_banks = [psum.tile([P, PACK, P], F32, name="own%d" % h) for h in range(HALVES)]
+        pairs = (("vector", 0), ("scalar", 2))
+        for a in range(PASSES):
+            codes = keep.tile([P, PACK, P], U32, name="w0_codes%d" % a, align_bytes=64)
+            scales = keep.tile([P, PACK, P], U8, name="w0_scales%d" % a, align_bytes=64)
+            pieces = 1 if a == 0 else 2
+            count = P // pieces
+            for piece in range(pieces):
+                raw = load_rows(w0, a, slice(piece * count * PACK, (piece + 1) * count * PACK))
+                dealt = raw[:].rearrange("p j (m t) -> p m j t", t=PACK)
+                shares = []
+                for engine, t0 in pairs:
+                    if a == 1 and piece == 0:
+                        engine = "scalar"
+                    grouped = keep.tile(
+                        [P, 2, count, PACK], BF16, name="w0_%d_%d_%d" % (a, piece, t0), align_bytes=64
+                    )
+                    copy_on(engine, grouped[:].rearrange("p t m j -> p m j t"), dealt[:, :, :, t0 : t0 + 2])
+                    shares.append((t0, grouped))
+                rows = slice(piece * count, (piece + 1) * count)
+                for t0, grouped in shares:
+                    if pieces == 1:
+                        quantize(
+                            codes[:, t0 : t0 + 2, :].rearrange("p t m -> p (t m)"),
+                            scales[:, t0 : t0 + 2, :].rearrange("p t m -> p (t m)"),
+                            grouped[:].rearrange("p t m j -> p (t m j)"),
+                        )
+                    else:
+                        for u in range(2):
+                            quantize(
+                                codes[:, t0 + u, rows],
+                                scales[:, t0 + u, rows],
+                                grouped[:, u, :, :].rearrange("p m j -> p (m j)"),
+                            )
+            for t0 in (0, 2):
+                for h in range(HALVES):
+                    for t in (t0, t0 + 1):
+                        picked = slice(h * P, (h + 1) * P)
+                        nc.tensor.matmul_mx(
+                            out=own_banks[h][:, t, :],
+                            lhsT=codes[:, t, :].bitcast(FP8X4),
+                            lhsT_scale=scales[:, t, :],
+                            rhs=x_codes[a][:, picked].bitcast(FP8X4),
+                            rhs_scale=x_planes[:, a, picked],
+                            start=(a == 0 and t == 0),
+                            stop=(a == PASSES - 1 and t == PACK - 1),
+                        )
+
+        turned = []
+        for h in range(HALVES):
+            gated = keep.tile([P, PACK, P], F32, name="gated%d" % h)
+            nc.scalar.copy(out=gated[:], in_=turned_banks[h][:])
+            turned.append(gated)
+
+        out_rows = out_0.rearrange("(p t) v -> p t v", t=PACK)
+        results = []
+        for h in range(HALVES):
+            result = keep.tile([P, PACK, P], F32, name="result%d" % h)
+            nc.vector.tensor_tensor(out=result[:], in0=own_banks[h][:], in1=turned[h][:], op=ADD)
+            nc.sync.dma_start(out=out_rows[:, :, h * P : (h + 1) * P], in_=result[:])
+            results.append(result)
+
+        y_codes = keep.tile([P, V], U32, name="y_codes", align_bytes=64)
+        y_scales = keep.tile([P, V], U8, name="y_scales", align_bytes=64)
+        rounded = []
+        for h, engine in enumerate(("scalar", "vector")):
+            grouped = keep.tile([P, P, PACK], BF16, name="y_grouped%d" % h, align_bytes=64)
+            copy_on(
+                engine,
+                grouped[:].rearrange("p (c i) t -> p c t i", i=4),
+                results[h][:].rearrange("p t (c i) -> p c t i", i=4),
+            )
+            rounded.append(grouped)
+        for h in range(HALVES):
+            cols = slice(h * P, (h + 1) * P)
+            quantize(y_codes[:, cols], y_scales[:, cols], rounded[h][:].rearrange("p c t -> p (c t)"))
+
+        nc.sync.dma_start(
+            out=out_1[0].rearrange("p n t -> p (n t)").bitcast(I32), in_=y_codes[:].bitcast(I32)
+        )
+        for q in range(QUADS):
+            queue = nc.scalar if q % 2 == 0 else nc.sync
+            queue.dma_start(
+                out=out_2[0].bitcast(I32)[4 * q : 4 * q + 4, :],
+                in_=y_scales[:].bitcast(I32)[32 * q : 32 * q + 4, :],
+            )

@@ -22,7 +22,8 @@ K_PASS = P * PACK
 PASSES = K // K_PASS
 HALVES = V // P
 QUADS = 4
-RAW_BUFS = 4
+SLOT = PACK * N * 4
+RAW_SLOTS = (4, 0, 1, 2, 3, 4, 0, 1, 2)
 SCALAR_COLS = 384
 SCALAR_COLS_LAST = 256
 
@@ -33,29 +34,30 @@ def tile_picked_zrgcn_none_po_kernel(
     nc = tc.nc
     with ExitStack() as ctx:
         keep = ctx.enter_context(tc.tile_pool(name="keep", bufs=1))
-        ring = ctx.enter_context(tc.tile_pool(name="ring", bufs=RAW_BUFS))
+        stage = ctx.enter_context(tc.tile_pool(name="stage", bufs=1))
         psum = ctx.enter_context(tc.psum_pool(name="psum", bufs=1))
 
         offsets = keep.tile([P, S // 16], U16, name="offsets")
         nc.sync.dma_start(offsets[:], offs)
 
-        scale_table = keep.tile([P, T], U8, name="scale_table", align_bytes=64)
-        nc.vector.memset(scale_table[:].bitcast(I32), 0)
-        nc.scalar.dma_start(
-            out=scale_table[:].bitcast(I32)[0:P:4, :],
+        scale_table = stage.tile([P, T], U8, name="scale_table", offset=4 * SLOT)
+        nc.sync.dma_start(
+            out=scale_table[:].bitcast(I32)[64:96, :],
             in_=x_scales.bitcast(I32).rearrange("a q c -> q a c"),
         )
+        nc.vector.memset(scale_table[:].bitcast(I32)[0:64, :], 0)
+        nc.vector.memset(scale_table[:].bitcast(I32)[96:128, :], 0)
 
         gate_rows = keep.tile([P, V], F32, name="gate_rows")
         nc.vector.memset(gate_rows[:], 0.0)
-        nc.scalar.dma_start(out=gate_rows[0:D, :], in_=gate[:, 0, :])
+        nc.sync.dma_start(out=gate_rows[0:D, :], in_=gate[:, 0, :])
 
         x_planes = keep.tile([P, PASSES, S], U8, name="x_planes", align_bytes=64)
         nc.vector.memset(x_planes[:].rearrange("p a s -> p (a s)").bitcast(I32), 0)
 
         word_tables = []
         for a in range(PASSES):
-            table = keep.tile([P, T], I32, name="word_table%d" % a, align_bytes=64)
+            table = stage.tile([P, T], I32, name="word_table%d" % a, offset=2 * a * SLOT)
             nc.sync.dma_start(out=table[:], in_=x_words[a].rearrange("p n t -> p (n t)").bitcast(I32))
             word_tables.append(table)
 
@@ -65,9 +67,9 @@ def tile_picked_zrgcn_none_po_kernel(
         picked_scales = keep.tile([P, S], U8, name="picked_scales", align_bytes=64)
         nc.vector.tensor_copy(picked_scales[:], scale_table[:].indirect(offsets[:]))
         for q in range(QUADS):
-            nc.gpsimd.dma_start(
+            nc.sync.dma_start(
                 out=x_planes[:].rearrange("p a s -> p (a s)").bitcast(I32)[32 * q : 32 * q + 4, :],
-                in_=picked_scales[:].bitcast(I32)[32 * q : 32 * (q + 1) : 4, :],
+                in_=picked_scales[:].bitcast(I32)[64 + 8 * q : 64 + 8 * (q + 1), :],
             )
 
         x_codes = []
@@ -82,9 +84,12 @@ def tile_picked_zrgcn_none_po_kernel(
         gate_cols = keep.tile([P, HALVES, D], F32, name="gate_cols")
         nc.scalar.copy(out=gate_cols[:], in_=gate_bank[:, :, 0:D])
 
+        raws = []
+
         def load_rows(w, a, cols):
             width = cols.stop - cols.start
-            raw = ring.tile([P, PACK, width], F32, name="raw")
+            raw = stage.tile([P, PACK, width], F32, name="raw%d" % len(raws), offset=RAW_SLOTS[len(raws)] * SLOT)
+            raws.append(raw)
             rows = w[a * K_PASS : (a + 1) * K_PASS, :].rearrange("(p j) c -> p j c", j=PACK)
             nc.sync.dma_start(out=raw[:], in_=rows[:, :, cols])
             return raw
@@ -155,7 +160,7 @@ def tile_picked_zrgcn_none_po_kernel(
             count = P // pieces
             for piece in range(pieces):
                 raw = load_rows(w0, a, slice(piece * count * PACK, (piece + 1) * count * PACK))
-                dealt = raw[:].rearrange("p j (m t) -> p m j t", t=PACK)
+                dealt = raw[:].rearrange("p j (m t) -> p m t j", t=PACK)
                 shares = []
                 for engine, t0 in pairs:
                     if a == 1 and piece == 0:
@@ -163,7 +168,7 @@ def tile_picked_zrgcn_none_po_kernel(
                     grouped = keep.tile(
                         [P, 2, count, PACK], BF16, name="w0_%d_%d_%d" % (a, piece, t0), align_bytes=64
                     )
-                    copy_on(engine, grouped[:].rearrange("p t m j -> p m j t"), dealt[:, :, :, t0 : t0 + 2])
+                    copy_on(engine, grouped[:].rearrange("p t m j -> p m t j"), dealt[:, :, t0 : t0 + 2, :])
                     shares.append((t0, grouped))
                 rows = slice(piece * count, (piece + 1) * count)
                 for t0, grouped in shares:

@@ -13,8 +13,8 @@ U32 = mybir.dt.uint32
 U16 = mybir.dt.uint16
 U8 = mybir.dt.uint8
 FP8X4 = mybir.dt.float8_e4m3fn_x4
-MULT = mybir.AluOpType.mult
 ADD = mybir.AluOpType.add
+COPY = mybir.ActivationFunctionType.Copy
 
 P = 128
 PACK = 4
@@ -24,8 +24,6 @@ HALVES = V // P
 QUADS = 4
 SLOT = PACK * N * 4
 RAW_SLOTS = (4, 0, 1, 2, 3, 4, 0, 1, 2)
-SCALAR_COLS = 384
-SCALAR_COLS_LAST = 256
 
 
 def tile_picked_zrgcn_none_po_kernel(
@@ -78,7 +76,7 @@ def tile_picked_zrgcn_none_po_kernel(
             nc.vector.tensor_copy(picked[:], word_tables[a][:].bitcast(U32).indirect(offsets[:]))
             x_codes.append(picked)
 
-        gate_bank = psum.tile([P, HALVES, P], F32, name="gate_bank")
+        gate_bank = psum.tile([P, HALVES, P], F32, name="gate_bank", tag="own0")
         for h in range(HALVES):
             nc.tensor.transpose(gate_bank[:, h, :], gate_rows[:, h * P : (h + 1) * P], identity[:])
         gate_cols = keep.tile([P, HALVES, D], F32, name="gate_cols")
@@ -103,115 +101,137 @@ def tile_picked_zrgcn_none_po_kernel(
         def quantize(codes, scales, in_):
             nc.vector.quantize_mx(out=codes.bitcast(FP8X4), scales=scales, in_=in_)
 
-        sums = [keep.tile([P, PACK, P], F32, name="sums%d" % h) for h in range(HALVES)]
-        for d, w in ((1, w1), (2, w2), (3, w3)):
+        turned_banks = [psum.tile([P, PACK, P], F32, name="turned%d" % h) for h in range(HALVES)]
+
+        last_codes = []
+
+        def gated_product(d, w):
             banks = [psum.tile([P, N], F32, name="part", tag="part%d_%d" % (d % 2, h)) for h in range(HALVES)]
             for a in range(PASSES):
                 raw = load_rows(w, a, slice(0, N))
                 codes = keep.tile([P, N], U32, name="w%d_codes%d" % (d, a), align_bytes=64)
                 scales = keep.tile([P, N], U8, name="w%d_scales%d" % (d, a), align_bytes=64)
-                split = SCALAR_COLS_LAST if (d, a) == (D, PASSES - 1) else SCALAR_COLS
-                shares = []
-                for engine, cols in (("vector", slice(split, N)), ("scalar", slice(0, split))):
-                    width = cols.stop - cols.start
-                    grouped = keep.tile([P, width, PACK], BF16, name="w%d_%d_%s" % (d, a, engine), align_bytes=64)
+                last = a == PASSES - 1
+                split = N // 2 if last or d == 1 else 0
+                grouped = keep.tile([P, N, PACK], BF16, name="w%d_grouped%d" % (d, a), align_bytes=64)
+                jobs = [("vector", slice(split, N))] + ([("scalar", slice(0, split))] if split else [])
+                for engine, cols in jobs:
                     copy_on(
                         engine,
-                        grouped[:].rearrange("p (c i) j -> p c j i", i=4),
+                        grouped[:, cols, :].rearrange("p (c i) j -> p c j i", i=4),
                         raw[:, :, cols].rearrange("p j (c i) -> p c j i", i=4),
                     )
-                    shares.append((cols, grouped))
-                for cols, grouped in shares:
-                    quantize(codes[:, cols], scales[:, cols], grouped[:].rearrange("p c j -> p (c j)"))
-                for h in range(HALVES):
-                    picked = slice(d * V + h * P, d * V + (h + 1) * P)
-                    nc.tensor.matmul_mx(
-                        out=banks[h][:],
-                        lhsT=x_codes[a][:, picked].bitcast(FP8X4),
-                        lhsT_scale=x_planes[:, a, picked],
-                        rhs=codes[:].bitcast(FP8X4),
-                        rhs_scale=scales[:],
-                        start=(a == 0),
-                        stop=(a == PASSES - 1),
-                    )
-            for h in range(HALVES):
-                product = banks[h][:].rearrange("p (m t) -> p t m", t=PACK)
-                weight = gate_cols[:, h, d - 1 : d]
-                if d == 1:
-                    nc.vector.tensor_scalar(out=sums[h][:], in0=product, scalar1=weight, scalar2=None, op0=MULT)
-                else:
-                    nc.vector.scalar_tensor_tensor(
-                        out=sums[h][:], in0=product, scalar=weight, in1=sums[h][:], op0=MULT, op1=ADD
-                    )
-
-        turned_banks = []
-        for h in range(HALVES):
-            bank = psum.tile([P, PACK, P], F32, name="turned", tag="part0_%d" % h)
-            for t in range(PACK):
-                nc.tensor.transpose(bank[:, t, :], sums[h][:, t, :], identity[:])
-            turned_banks.append(bank)
-
-        own_banks = [psum.tile([P, PACK, P], F32, name="own%d" % h) for h in range(HALVES)]
-        pairs = (("vector", 0), ("scalar", 2))
-        for a in range(PASSES):
-            codes = keep.tile([P, PACK, P], U32, name="w0_codes%d" % a, align_bytes=64)
-            scales = keep.tile([P, PACK, P], U8, name="w0_scales%d" % a, align_bytes=64)
-            pieces = 1 if a == 0 else 2
-            count = P // pieces
-            for piece in range(pieces):
-                raw = load_rows(w0, a, slice(piece * count * PACK, (piece + 1) * count * PACK))
-                dealt = raw[:].rearrange("p j (m t) -> p m t j", t=PACK)
-                shares = []
-                for engine, t0 in pairs:
-                    if a == 1 and piece == 0:
-                        engine = "scalar"
-                    grouped = keep.tile(
-                        [P, 2, count, PACK], BF16, name="w0_%d_%d_%d" % (a, piece, t0), align_bytes=64
-                    )
-                    copy_on(engine, grouped[:].rearrange("p t m j -> p m t j"), dealt[:, :, t0 : t0 + 2, :])
-                    shares.append((t0, grouped))
-                rows = slice(piece * count, (piece + 1) * count)
-                for t0, grouped in shares:
-                    if pieces == 1:
-                        quantize(
-                            codes[:, t0 : t0 + 2, :].rearrange("p t m -> p (t m)"),
-                            scales[:, t0 : t0 + 2, :].rearrange("p t m -> p (t m)"),
-                            grouped[:].rearrange("p t m j -> p (t m j)"),
-                        )
-                    else:
-                        for u in range(2):
-                            quantize(
-                                codes[:, t0 + u, rows],
-                                scales[:, t0 + u, rows],
-                                grouped[:, u, :, :].rearrange("p m j -> p (m j)"),
-                            )
-            for t0 in (0, 2):
-                for h in range(HALVES):
-                    for t in (t0, t0 + 1):
-                        picked = slice(h * P, (h + 1) * P)
+                spans = [slice(split, N), slice(0, split)] if last else [slice(0, N)]
+                for cols in spans:
+                    quantize(codes[:, cols], scales[:, cols], grouped[:, cols, :].rearrange("p c j -> p (c j)"))
+                for cols in spans:
+                    for h in range(HALVES):
+                        picked = slice(d * V + h * P, d * V + (h + 1) * P)
                         nc.tensor.matmul_mx(
-                            out=own_banks[h][:, t, :],
-                            lhsT=codes[:, t, :].bitcast(FP8X4),
-                            lhsT_scale=scales[:, t, :],
-                            rhs=x_codes[a][:, picked].bitcast(FP8X4),
-                            rhs_scale=x_planes[:, a, picked],
-                            start=(a == 0 and t == 0),
-                            stop=(a == PASSES - 1 and t == PACK - 1),
+                            out=banks[h][:, cols],
+                            lhsT=x_codes[a][:, picked].bitcast(FP8X4),
+                            lhsT_scale=x_planes[:, a, picked],
+                            rhs=codes[:, cols].bitcast(FP8X4),
+                            rhs_scale=scales[:, cols],
+                            start=(a == 0),
+                            stop=(a == PASSES - 1 and cols == spans[-1]),
                         )
+            last_codes.append(codes)
+            return banks
+
+        def add_gated(d, h, bank):
+            scaled = keep.tile([P, PACK, P], F32, name="scaled%d_%d" % (d, h))
+            nc.scalar.activation(
+                out=scaled[:],
+                in_=bank[:].rearrange("p (m t) -> p t m", t=PACK),
+                func=COPY,
+                scale=gate_cols[:, h, d - 1 : d],
+            )
+            for t in range(PACK):
+                nc.tensor.matmul(
+                    turned_banks[h][:, t, :],
+                    scaled[:, t, :],
+                    identity[:],
+                    start=(d == 1 and t == 0),
+                    stop=(d == D and t == PACK - 1),
+                    is_transpose=True,
+                )
+
+
+        def own_round(a, jobs):
+            raw = load_rows(w0, a, slice(0, N))
+            dealt = raw[:].rearrange("p j (m t) -> p m t j", t=PACK)
+            pairs = [
+                keep.tile([P, 2, P, PACK], BF16, name="w0_grouped%d_%d" % (a, pair), align_bytes=64)
+                for pair in range(2)
+            ]
+            for engine, pair, rows in jobs:
+                copy_on(
+                    engine,
+                    pairs[pair][:].rearrange("p t m j -> p m t j")[:, rows, :, :],
+                    dealt[:, rows, 2 * pair : 2 * pair + 2, :],
+                )
+            return pairs
+
+        def own_product(a, pair, grouped):
+            t0 = 2 * pair
+            codes, scales = own_codes[a], own_scales[a]
+            quantize(
+                codes[:, t0 : t0 + 2, :].rearrange("p t m -> p (t m)"),
+                scales[:, t0 : t0 + 2, :].rearrange("p t m -> p (t m)"),
+                grouped[:].rearrange("p t m j -> p (t m j)"),
+            )
+            for h in range(HALVES):
+                for t in (t0, t0 + 1):
+                    picked = slice(h * P, (h + 1) * P)
+                    nc.tensor.matmul_mx(
+                        out=own_banks[pair][h][:, t - t0, :],
+                        lhsT=codes[:, t, :].bitcast(FP8X4),
+                        lhsT_scale=scales[:, t, :],
+                        rhs=x_codes[a][:, picked].bitcast(FP8X4),
+                        rhs_scale=x_planes[:, a, picked],
+                        start=(a == 0 and t == t0),
+                        stop=(a == PASSES - 1 and t == t0 + 1),
+                    )
+
+        for d, w in ((1, w1), (2, w2), (3, w3)):
+            banks = gated_product(d, w)
+            for h in range(HALVES):
+                add_gated(d, h, banks[h])
+
+        own_banks = [
+            [psum.tile([P, 2, P], F32, name="own", tag=tag % h) for h in range(HALVES)] for tag in ("own%d", "part0_%d")
+        ]
+        own_codes = [keep.tile([P, PACK, P], U32, name="w0_codes%d" % a, align_bytes=64) for a in range(PASSES)]
+        own_scales = [keep.tile([P, PACK, P], U8, name="w0_scales%d" % a, align_bytes=64) for a in range(PASSES)]
+
+        whole = slice(0, P)
+        pairs = own_round(0, (("vector", 0, whole), ("vector", 1, whole)))
+        own_product(0, 0, pairs[0])
+        own_product(0, 1, pairs[1])
+
+        pairs = own_round(
+            1, (("vector", 0, whole), ("vector", 1, slice(0, P // 4)), ("scalar", 1, slice(P // 4, P)))
+        )
+        own_product(1, 0, pairs[0])
+        own_product(1, 1, pairs[1])
 
         turned = []
         for h in range(HALVES):
-            gated = keep.tile([P, PACK, P], F32, name="gated%d" % h)
+            gated = stage.tile([P, PACK, P], F32, name="gated%d" % h, offset=RAW_SLOTS[7] * SLOT + h * PACK * P * 4)
             nc.scalar.copy(out=gated[:], in_=turned_banks[h][:])
             turned.append(gated)
 
         out_rows = out_0.rearrange("(p t) v -> p t v", t=PACK)
-        results = []
+        results = [keep.tile([P, PACK, P], F32, name="result%d" % h) for h in range(HALVES)]
+        for pair in range(2):
+            rows = slice(2 * pair, 2 * pair + 2)
+            for h in range(HALVES):
+                nc.vector.tensor_tensor(
+                    out=results[h][:, rows, :], in0=own_banks[pair][h][:], in1=turned[h][:, rows, :], op=ADD
+                )
         for h in range(HALVES):
-            result = keep.tile([P, PACK, P], F32, name="result%d" % h)
-            nc.vector.tensor_tensor(out=result[:], in0=own_banks[h][:], in1=turned[h][:], op=ADD)
-            nc.sync.dma_start(out=out_rows[:, :, h * P : (h + 1) * P], in_=result[:])
-            results.append(result)
+            nc.sync.dma_start(out=out_rows[:, :, h * P : (h + 1) * P], in_=results[h][:])
 
         y_codes = keep.tile([P, V], U32, name="y_codes", align_bytes=64)
         y_scales = keep.tile([P, V], U8, name="y_scales", align_bytes=64)

@@ -35,9 +35,6 @@ def tile_picked_zrgcn_none_po_kernel(
         stage = ctx.enter_context(tc.tile_pool(name="stage", bufs=1))
         psum = ctx.enter_context(tc.psum_pool(name="psum", bufs=1))
 
-        offsets = keep.tile([P, S // 16], U16, name="offsets")
-        nc.sync.dma_start(offsets[:], offs)
-
         scale_table = stage.tile([P, T], U8, name="scale_table", offset=4 * SLOT)
         nc.sync.dma_start(
             out=scale_table[:].bitcast(I32)[64:96, :],
@@ -45,6 +42,9 @@ def tile_picked_zrgcn_none_po_kernel(
         )
         nc.vector.memset(scale_table[:].bitcast(I32)[0:64, :], 0)
         nc.vector.memset(scale_table[:].bitcast(I32)[96:128, :], 0)
+
+        offsets = keep.tile([P, S // 16], U16, name="offsets")
+        nc.sync.dma_start(offsets[:], offs)
 
         gate_rows = keep.tile([P, V], F32, name="gate_rows")
         nc.vector.memset(gate_rows[:], 0.0)
@@ -160,7 +160,7 @@ def tile_picked_zrgcn_none_po_kernel(
 
         def own_round(a, jobs):
             raw = load_rows(w0, a, slice(0, N))
-            dealt = raw[:].rearrange("p j (m t) -> p m t j", t=PACK)
+            dealt = raw[:].rearrange("p j (m t) -> p m j t", t=PACK)
             pairs = [
                 keep.tile([P, 2, P, PACK], BF16, name="w0_grouped%d_%d" % (a, pair), align_bytes=64)
                 for pair in range(2)
@@ -168,8 +168,8 @@ def tile_picked_zrgcn_none_po_kernel(
             for engine, pair, rows in jobs:
                 copy_on(
                     engine,
-                    pairs[pair][:].rearrange("p t m j -> p m t j")[:, rows, :, :],
-                    dealt[:, rows, 2 * pair : 2 * pair + 2, :],
+                    pairs[pair][:].rearrange("p t m j -> p m j t")[:, rows, :, :],
+                    dealt[:, rows, :, 2 * pair : 2 * pair + 2],
                 )
             return pairs
 
@@ -206,7 +206,9 @@ def tile_picked_zrgcn_none_po_kernel(
         own_scales = [keep.tile([P, PACK, P], U8, name="w0_scales%d" % a, align_bytes=64) for a in range(PASSES)]
 
         whole = slice(0, P)
-        pairs = own_round(0, (("vector", 0, whole), ("vector", 1, whole)))
+        pairs = own_round(
+            0, (("vector", 0, whole), ("vector", 1, slice(0, 3 * P // 4)), ("scalar", 1, slice(3 * P // 4, P)))
+        )
         own_product(0, 0, pairs[0])
         own_product(0, 1, pairs[1])
 
@@ -223,15 +225,17 @@ def tile_picked_zrgcn_none_po_kernel(
             turned.append(gated)
 
         out_rows = out_0.rearrange("(p t) v -> p t v", t=PACK)
-        results = [keep.tile([P, PACK, P], F32, name="result%d" % h) for h in range(HALVES)]
+        result = keep.tile([P, PACK, V], F32, name="result")
         for pair in range(2):
             rows = slice(2 * pair, 2 * pair + 2)
             for h in range(HALVES):
                 nc.vector.tensor_tensor(
-                    out=results[h][:, rows, :], in0=own_banks[pair][h][:], in1=turned[h][:, rows, :], op=ADD
+                    out=result[:, rows, h * P : (h + 1) * P],
+                    in0=own_banks[pair][h][:],
+                    in1=turned[h][:, rows, :],
+                    op=ADD,
                 )
-        for h in range(HALVES):
-            nc.sync.dma_start(out=out_rows[:, :, h * P : (h + 1) * P], in_=results[h][:])
+            nc.sync.dma_start(out=out_rows[:, rows, :], in_=result[:, rows, :])
 
         y_codes = keep.tile([P, V], U32, name="y_codes", align_bytes=64)
         y_scales = keep.tile([P, V], U8, name="y_scales", align_bytes=64)
@@ -241,7 +245,7 @@ def tile_picked_zrgcn_none_po_kernel(
             copy_on(
                 engine,
                 grouped[:].rearrange("p (c i) t -> p c t i", i=4),
-                results[h][:].rearrange("p t (c i) -> p c t i", i=4),
+                result[:, :, h * P : (h + 1) * P].rearrange("p t (c i) -> p c t i", i=4),
             )
             rounded.append(grouped)
         for h in range(HALVES):

from contextlib import ExitStack

import concourse.mybir as mybir
from concourse.masks import make_identity

K, T, S, V, D, N = 1024, 4096, 1024, 256, 3, 512
FLOPS = 2 * (D + 1) * K * N * V

F32 = mybir.dt.float32
BF16 = mybir.dt.bfloat16
I32 = mybir.dt.int32
U32 = mybir.dt.uint32
U16 = mybir.dt.uint16
U8 = mybir.dt.uint8
FP8X4 = mybir.dt.float8_e4m3fn_x4
ADD = mybir.AluOpType.add
COPY = mybir.ActivationFunctionType.Copy

P = 128
PACK = 4
K_PASS = P * PACK
PASSES = K // K_PASS
HALVES = V // P
QUADS = 4
SLOT = PACK * N * 4
RAW_SLOTS = (4, 0, 1, 2, 3, 4, 0, 1, 2)


def tile_picked_zrgcn_none_po_kernel(
    tc, x_words, x_scales, w0, w1, w2, w3, gate, offs, out_0, out_1, out_2
):
    nc = tc.nc
    with ExitStack() as ctx:
        keep = ctx.enter_context(tc.tile_pool(name="keep", bufs=1))
        stage = ctx.enter_context(tc.tile_pool(name="stage", bufs=1))
        psum = ctx.enter_context(tc.psum_pool(name="psum", bufs=1))

        scale_table = stage.tile([P, T], U8, name="scale_table", offset=4 * SLOT)
        nc.sync.dma_start(
            out=scale_table[:].bitcast(I32)[64:96, :],
            in_=x_scales.bitcast(I32).rearrange("a q c -> q a c"),
        )
        nc.vector.memset(scale_table[:].bitcast(I32)[0:64, :], 0)
        nc.vector.memset(scale_table[:].bitcast(I32)[96:128, :], 0)

        offsets = keep.tile([P, S // 16], U16, name="offsets")
        nc.sync.dma_start(offsets[:], offs)

        gate_rows = keep.tile([P, V], F32, name="gate_rows")
        nc.vector.memset(gate_rows[:], 0.0)
        nc.sync.dma_start(out=gate_rows[0:D, :], in_=gate[:, 0, :])

        x_planes = keep.tile([P, PASSES, S], U8, name="x_planes", align_bytes=64)
        nc.vector.memset(x_planes[:].rearrange("p a s -> p (a s)").bitcast(I32), 0)

        word_tables = []
        for a in range(PASSES):
            table = stage.tile([P, T], I32, name="word_table%d" % a, offset=2 * a * SLOT)
            nc.sync.dma_start(out=table[:], in_=x_words[a].rearrange("p n t -> p (n t)").bitcast(I32))
            word_tables.append(table)

        identity = keep.tile([P, P], F32, name="identity")
        make_identity(nc, identity[:])

        picked_scales = keep.tile([P, S], U8, name="picked_scales", align_bytes=64)
        nc.vector.tensor_copy(picked_scales[:], scale_table[:].indirect(offsets[:]))
        for q in range(QUADS):
            nc.sync.dma_start(
                out=x_planes[:].rearrange("p a s -> p (a s)").bitcast(I32)[32 * q : 32 * q + 4, :],
                in_=picked_scales[:].bitcast(I32)[64 + 8 * q : 64 + 8 * (q + 1), :],
            )

        x_codes = []
        for a in range(PASSES):
            picked = keep.tile([P, S], U32, name="x_codes%d" % a, align_bytes=64)
            nc.vector.tensor_copy(picked[:], word_tables[a][:].bitcast(U32).indirect(offsets[:]))
            x_codes.append(picked)

        gate_bank = psum.tile([P, HALVES, P], F32, name="gate_bank", tag="own0")
        for h in range(HALVES):
            nc.tensor.transpose(gate_bank[:, h, :], gate_rows[:, h * P : (h + 1) * P], identity[:])
        gate_cols = keep.tile([P, HALVES, D], F32, name="gate_cols")
        nc.scalar.copy(out=gate_cols[:], in_=gate_bank[:, :, 0:D])

        raws = []

        def load_rows(w, a, cols):
            width = cols.stop - cols.start
            raw = stage.tile([P, PACK, width], F32, name="raw%d" % len(raws), offset=RAW_SLOTS[len(raws)] * SLOT)
            raws.append(raw)
            rows = w[a * K_PASS : (a + 1) * K_PASS, :].rearrange("(p j) c -> p j c", j=PACK)
            nc.sync.dma_start(out=raw[:], in_=rows[:, :, cols])
            return raw

        def copy_on(engine, out, in_):
            if engine == "scalar":
                nc.scalar.copy(out=out, in_=in_)
            else:
                nc.vector.tensor_copy(out=out, in_=in_)

        def quantize(codes, scales, in_):
            nc.vector.quantize_mx(out=codes.bitcast(FP8X4), scales=scales, in_=in_)

        turned_banks = [psum.tile([P, PACK, P], F32, name="turned%d" % h) for h in range(HALVES)]

        last_codes = []

        def gated_product(d, w):
            banks = [psum.tile([P, N], F32, name="part", tag="part%d_%d" % (d % 2, h)) for h in range(HALVES)]
            for a in range(PASSES):
                raw = load_rows(w, a, slice(0, N))
                codes = keep.tile([P, N], U32, name="w%d_codes%d" % (d, a), align_bytes=64)
                scales = keep.tile([P, N], U8, name="w%d_scales%d" % (d, a), align_bytes=64)
                last = a == PASSES - 1
                split = N // 2 if last or d == 1 else 0
                grouped = keep.tile([P, N, PACK], BF16, name="w%d_grouped%d" % (d, a), align_bytes=64)
                jobs = [("vector", slice(split, N))] + ([("scalar", slice(0, split))] if split else [])
                for engine, cols in jobs:
                    copy_on(
                        engine,
                        grouped[:, cols, :].rearrange("p (c i) j -> p c j i", i=4),
                        raw[:, :, cols].rearrange("p j (c i) -> p c j i", i=4),
                    )
                spans = [slice(split, N), slice(0, split)] if last else [slice(0, N)]
                for cols in spans:
                    quantize(codes[:, cols], scales[:, cols], grouped[:, cols, :].rearrange("p c j -> p (c j)"))
                for cols in spans:
                    for h in range(HALVES):
                        picked = slice(d * V + h * P, d * V + (h + 1) * P)
                        nc.tensor.matmul_mx(
                            out=banks[h][:, cols],
                            lhsT=x_codes[a][:, picked].bitcast(FP8X4),
                            lhsT_scale=x_planes[:, a, picked],
                            rhs=codes[:, cols].bitcast(FP8X4),
                            rhs_scale=scales[:, cols],
                            start=(a == 0),
                            stop=(a == PASSES - 1 and cols == spans[-1]),
                        )
            last_codes.append(codes)
            return banks

        def add_gated(d, h, bank):
            scaled = keep.tile([P, PACK, P], F32, name="scaled%d_%d" % (d, h))
            nc.scalar.activation(
                out=scaled[:],
                in_=bank[:].rearrange("p (m t) -> p t m", t=PACK),
                func=COPY,
                scale=gate_cols[:, h, d - 1 : d],
            )
            for t in range(PACK):
                nc.tensor.matmul(
                    turned_banks[h][:, t, :],
                    scaled[:, t, :],
                    identity[:],
                    start=(d == 1 and t == 0),
                    stop=(d == D and t == PACK - 1),
                    is_transpose=True,
                )


        def own_round(a, jobs):
            raw = load_rows(w0, a, slice(0, N))
            dealt = raw[:].rearrange("p j (m t) -> p m j t", t=PACK)
            pairs = [
                keep.tile([P, 2, P, PACK], BF16, name="w0_grouped%d_%d" % (a, pair), align_bytes=64)
                for pair in range(2)
            ]
            for engine, pair, rows in jobs:
                copy_on(
                    engine,
                    pairs[pair][:].rearrange("p t m j -> p m j t")[:, rows, :, :],
                    dealt[:, rows, :, 2 * pair : 2 * pair + 2],
                )
            return pairs

        def own_product(a, pair, grouped):
            t0 = 2 * pair
            codes, scales = own_codes[a], own_scales[a]
            quantize(
                codes[:, t0 : t0 + 2, :].rearrange("p t m -> p (t m)"),
                scales[:, t0 : t0 + 2, :].rearrange("p t m -> p (t m)"),
                grouped[:].rearrange("p t m j -> p (t m j)"),
            )
            for h in range(HALVES):
                for t in (t0, t0 + 1):
                    picked = slice(h * P, (h + 1) * P)
                    nc.tensor.matmul_mx(
                        out=own_banks[pair][h][:, t - t0, :],
                        lhsT=codes[:, t, :].bitcast(FP8X4),
                        lhsT_scale=scales[:, t, :],
                        rhs=x_codes[a][:, picked].bitcast(FP8X4),
                        rhs_scale=x_planes[:, a, picked],
                        start=(a == 0 and t == t0),
                        stop=(a == PASSES - 1 and t == t0 + 1),
                    )

        for d, w in ((1, w1), (2, w2), (3, w3)):
            banks = gated_product(d, w)
            for h in range(HALVES):
                add_gated(d, h, banks[h])

        own_banks = [
            [psum.tile([P, 2, P], F32, name="own", tag=tag % h) for h in range(HALVES)] for tag in ("own%d", "part0_%d")
        ]
        own_codes = [keep.tile([P, PACK, P], U32, name="w0_codes%d" % a, align_bytes=64) for a in range(PASSES)]
        own_scales = [keep.tile([P, PACK, P], U8, name="w0_scales%d" % a, align_bytes=64) for a in range(PASSES)]

        whole = slice(0, P)
        pairs = own_round(
            0, (("vector", 0, whole), ("vector", 1, slice(0, 3 * P // 4)), ("scalar", 1, slice(3 * P // 4, P)))
        )
        own_product(0, 0, pairs[0])
        own_product(0, 1, pairs[1])

        pairs = own_round(
            1, (("vector", 0, whole), ("vector", 1, slice(0, P // 4)), ("scalar", 1, slice(P // 4, P)))
        )
        own_product(1, 0, pairs[0])
        own_product(1, 1, pairs[1])

        turned = []
        for h in range(HALVES):
            gated = stage.tile([P, PACK, P], F32, name="gated%d" % h, offset=RAW_SLOTS[7] * SLOT + h * PACK * P * 4)
            nc.scalar.copy(out=gated[:], in_=turned_banks[h][:])
            turned.append(gated)

        out_rows = out_0.rearrange("(p t) v -> p t v", t=PACK)
        result = keep.tile([P, PACK, V], F32, name="result")
        for pair in range(2):
            rows = slice(2 * pair, 2 * pair + 2)
            for h in range(HALVES):
                nc.vector.tensor_tensor(
                    out=result[:, rows, h * P : (h + 1) * P],
                    in0=own_banks[pair][h][:],
                    in1=turned[h][:, rows, :],
                    op=ADD,
                )
            nc.sync.dma_start(out=out_rows[:, rows, :], in_=result[:, rows, :])

        y_codes = keep.tile([P, V], U32, name="y_codes", align_bytes=64)
        y_scales = keep.tile([P, V], U8, name="y_scales", align_bytes=64)
        rounded = []
        for h, engine in enumerate(("scalar", "vector")):
            grouped = keep.tile([P, P, PACK], BF16, name="y_grouped%d" % h, align_bytes=64)
            copy_on(
                engine,
                grouped[:].rearrange("p (c i) t -> p c t i", i=4),
                result[:, :, h * P : (h + 1) * P].rearrange("p t (c i) -> p c t i", i=4),
            )
            rounded.append(grouped)
        for h in range(HALVES):
            cols = slice(h * P, (h + 1) * P)
            quantize(y_codes[:, cols], y_scales[:, cols], rounded[h][:].rearrange("p c t -> p (c t)"))

        nc.sync.dma_start(
            out=out_1[0].rearrange("p n t -> p (n t)").bitcast(I32), in_=y_codes[:].bitcast(I32)
        )
        for q in range(QUADS):
            queue = nc.scalar if q % 2 == 0 else nc.sync
            queue.dma_start(
                out=out_2[0].bitcast(I32)[4 * q : 4 * q + 4, :],
                in_=y_scales[:].bitcast(I32)[32 * q : 32 * q + 4, :],
            )
